import numpy as np, ml_dtypes
CORES = [24,32,56,88,96,104,30,38,62,94,102,110]
N = 12
TK = 512
COEF = [[2,-1,0,0,0,0,1,0,0,0,0,-1],[-1,2,-1,0,0,0,0,1,0,0,0,0],[0,-1,2,-1,0,0,0,0,1,0,0,0],[0,0,-1,2,-1,0,0,0,0,1,0,0],[0,0,0,-1,2,-1,0,0,0,0,1,0],[0,0,0,0,-1,2,-1,0,0,0,0,1],[1,0,0,0,0,-1,2,-1,0,0,0,0],[0,1,0,0,0,0,-1,2,-1,0,0,0],[0,0,1,0,0,0,0,-1,2,-1,0,0],[0,0,0,1,0,0,0,0,-1,2,-1,0],[0,0,0,0,1,0,0,0,0,-1,2,-1],[-1,0,0,0,0,1,0,0,0,0,-1,2]]
def setup_inputs(rng):
    return {"x": rng.standard_normal((N, 128, TK), dtype=np.float32).astype(ml_dtypes.bfloat16), "a": (rng.standard_normal((N, 128, 128), dtype=np.float32) / 11).astype(ml_dtypes.bfloat16)}
def setup_inputs_big(rng):
    d = setup_inputs(rng)
    for k in ("x", "a"): d[k] = (d[k].astype(np.float32) * 1024.0).astype(d[k].dtype)
    return d
def setup_inputs_small(rng):
    d = setup_inputs(rng)
    for k in ("x", "a"): d[k] = (d[k].astype(np.float32) * (1 / 1024.0)).astype(d[k].dtype)
    return d
def setup_inputs_apart(rng):
    d = setup_inputs(rng)
    f = (10.0 ** rng.permutation(np.linspace(-1.5, 1.5, N))).astype(np.float32).reshape(N, 1, 1)
    for k in ("x", "a"): d[k] = (d[k].astype(np.float32) * f).astype(d[k].dtype)
    return d
def reference(x, a):
    X, A = x.astype(np.float64), a.astype(np.float64)
    y = np.stack([A[r].T @ sum(COEF[r][j] * X[j] for j in range(N)) for r in range(N)])
    return {"y": y.astype(ml_dtypes.bfloat16)}

@@ -1,0 +1,204 @@
+from concourse.bass import DstId, RemoteDMATransfer
+from concourse.mybir import AluOpType
+
+SIM_CORES = 112
+P, W, M = 128, 512, 128
+NCOL = 4
+NSC = 2
+HALVES = 2
+
+RELAY = "partner"
+SHARE = True
+HOME = 8
+CRIT_FIRST = False
+
+SCRATCH = {
+    "xs": ("sbuf", [P, W], "bfloat16"),
+    "a1": ("sbuf", [P, M], "bfloat16"),
+    "ysb": ("sbuf", [P, W], "bfloat16"),
+}
+for _i in range(NCOL):
+    SCRATCH["land%d" % _i] = ("sbuf", [P, W], "bfloat16")
+for _i in range(NSC):
+    SCRATCH["kc%d" % _i] = ("sbuf", [P, M], "bfloat16")
+    SCRATCH["as%d" % _i] = ("sbuf", [P, M], "bfloat16")
+for _i in range(HALVES):
+    SCRATCH["ps%d" % _i] = ("psum", [P, 512], "float32")
+
+SEMAPHORES = (["xl", "al", "ks", "aw", "sent"] + ["arr%d" % i for i in range(NCOL)]
+              + ["mm%d" % i for i in range(HALVES)] + ["cp%d" % i for i in range(HALVES)]
+              + ["st%d" % i for i in range(HALVES)])
+
+
+def _bits(mask):
+    return [b for b in range(mask.bit_length()) if (mask >> b) & 1]
+
+
+def _deal(ws, m):
+    if m == 1:
+        return [ws]
+    h = m // 2
+    return _deal(ws[0::2], h) + _deal(ws[1::2], m - h)
+
+
+def _plan(T, topo):
+    cores = list(T.cores)
+    n = len(cores)
+    coef = T.tables["COEF"]
+    group = set(cores)
+    need = {r: [j for j in range(n) if j != r and coef[r][j] != 0] for r in range(n)}
+    colour = {}
+    for j in range(n):
+        clash = set()
+        for r in range(n):
+            if j in need[r]:
+                clash |= {colour[i] for i in need[r] if i in colour and i != j}
+        c = 0
+        while c in clash:
+            c += 1
+        colour[j] = c
+    routes = {}
+    load = {}
+    edges = [(j, r) for r in range(n) for j in need[r]]
+    opts = {}
+    for (j, r) in edges:
+        s, d = cores[j], cores[r]
+        if topo.chip(s) == topo.chip(d):
+            routes[(j, r)] = [s, d]
+            continue
+        o = [s] if topo.may_write(s, d) else []
+        if RELAY == "helper":
+            if not o:
+                o = [h for h in range(SIM_CORES) if h not in group and topo.chip(h) == topo.chip(s)
+                     and topo.die(h) == topo.die(s) and topo.may_write(h, d)]
+        elif SHARE or not o:
+            o += [cores[q] for q in range(n) if j in need[q] and topo.chip(cores[q]) == topo.chip(s)
+                  and topo.may_write(cores[q], d)]
+        opts[(j, r)] = o
+    for e in sorted(opts, key=lambda e: (len(opts[e]) > 1 and RELAY != "helper", e)):
+        s, d = cores[e[0]], cores[e[1]]
+        h = min(opts[e], key=lambda c: (load.get(c, 0), c != s, c))
+        load[h] = load.get(h, 0) + 1
+        routes[e] = [s, d] if h == s else [s, h, d]
+    hops = {e: len(p) - 1 for e, p in routes.items()}
+    own, fwd = {}, {}
+    for (j, r), p in routes.items():
+        lst = own.setdefault(p[0], [])
+        hit = [t for t in lst if t[0] == p[1]]
+        if not hit:
+            hit = [[p[1], j, False]]
+            lst.append(hit[0])
+        if len(p) > 2:
+            hit[0][2] = True
+            fwd.setdefault(p[1], {}).setdefault(j, []).append(p[2])
+    calls = {}
+    for c, lst in own.items():
+        if CRIT_FIRST:
+            parts = [[t for t in lst if t[2]], [t for t in lst if not t[2]]]
+        else:
+            parts = [sorted(lst, key=lambda t: not t[2])]
+        for part in parts:
+            if part:
+                calls.setdefault(c, []).append(("x", part[0][1], [t[0] for t in part]))
+    for c, by in fwd.items():
+        for j in sorted(by):
+            calls.setdefault(c, []).append(("arr", j, by[j]))
+    far = {c: [d for d in cores if topo.chip(d) != topo.chip(c)][0] for c in calls}
+    out, income = {}, {}
+    for c, cl in calls.items():
+        lo = _bits(topo.mask(c, far[c]))
+        leaves = any(topo.chip(d) != topo.chip(c) for _k, _j, tos in cl for d in tos)
+        out[c] = []
+        for kind, j, tos in cl:
+            near = [d for d in tos if topo.chip(d) == topo.chip(c)]
+            away = [d for d in tos if topo.chip(d) != topo.chip(c)]
+            if not leaves:
+                every = _bits(topo.mask(c, near[0]))
+                give = dict(zip(tos, _deal(every[0::len(every) // HOME], len(tos))))
+            elif len(tos) <= 2 or not near:
+                give = dict(zip(tos, _deal(lo, len(tos))))
+            else:
+                hi = [b for b in _bits(topo.mask(c, near[0])) if b not in lo]
+                give = dict(zip(away, _deal(lo, len(away))))
+                give.update(zip(near, _deal(hi[0::2], len(near))))
+            trs = []
+            for d in tos:
+                trs.append((d, sum(1 << b for b in give[d]), len(give[d])))
+                income[(d, j)] = len(give[d])
+            out[c].append((kind, j, trs))
+    return need, colour, hops, out, income
+
+
+def rank_program(g, core, T, topo):
+    need, colour, hops, calls, income = _plan(T, topo)
+    rank = T.rank_of(core)
+    mine = calls.get(core, [])
+    if rank is None and not mine:
+        return
+    sem = T.sem
+
+    if rank is not None:
+        g.sync.dma_start(T.xs[:, :], T.x[:, :]).then_inc(sem.xl, 16)
+        g.sync.dma_start(T.a1[:, :], T.a[:, :]).then_inc(sem.al, 16)
+
+    sent = 0
+    for kind, j, trs in mine:
+        col = colour[j]
+        if kind == "x":
+            g.wait_ge(sem.xl, 16)
+            src = T.xs[:, :]
+        else:
+            g.wait_ge(sem["arr%d" % col], income[(core, j)])
+            src = T["land%d" % col][:, :]
+        lst = []
+        for d, mask, cnt in trs:
+            rid, pid, _se = topo.addr(d)
+            lst.append(RemoteDMATransfer(dst_ids=[DstId(rid=rid, pnc=pid)], dma_engine_mask=mask,
+                                         remote_sem=sem["arr%d" % col], src=src, dst=T["land%d" % col][:, :]))
+            sent += cnt
+        g.remote_dma_fused(lst, local_sem=sem.sent)
+    if sent:
+        g.wait_ge(sem.sent, sent)
+    if rank is None:
+        return
+
+    row = T.tables["COEF"][rank]
+    vals = sorted({row[j] for j in need[rank] + [rank]} - {1})
+    lhs = {1: T.a1}
+    for i, c in enumerate(vals):
+        g.vector.memset(T["kc%d" % i][:, :], float(c)).then_inc(sem.ks, 1)
+        lhs[c] = T["as%d" % i]
+    if vals:
+        g.vector.wait_ge(sem.ks, len(vals))
+        g.vector.wait_ge(sem.al, 16)
+        for i, c in enumerate(vals):
+            g.vector.tensor_tensor(T["as%d" % i][:, :], T.a1[:, :], T["kc%d" % i][:, :],
+                                   AluOpType.mult).then_inc(sem.aw, 1)
+
+    order = sorted(need[rank], key=lambda j: (hops[(j, rank)], topo.chip(T.cores[j]) != topo.chip(core),
+                                              -income[(core, j)], j))
+    hw = W // HALVES
+    g.tensor.wait_ge(sem.al, 16)
+    if vals:
+        g.tensor.wait_ge(sem.aw, len(vals))
+    g.tensor.wait_ge(sem.xl, 16)
+    for k, j in enumerate([rank] + order):
+        if j == rank:
+            blk = T.xs
+        else:
+            blk = T["land%d" % colour[j]]
+            g.tensor.wait_ge(sem["arr%d" % colour[j]], income[(core, j)])
+        last = k == len(order)
+        for h in range(HALVES):
+            mm = g.tensor.matmul(T["ps%d" % h][:, 0:hw], lhs[row[j]][:, :], blk[:, h * hw:(h + 1) * hw], k == 0, last)
+            if last:
+                mm.then_inc(sem["mm%d" % h], 1)
+
+    for h in range(HALVES):
+        g.vector.wait_ge(sem["mm%d" % h], 1)
+        g.vector.tensor_copy(T.ysb[:, h * hw:(h + 1) * hw], T["ps%d" % h][:, 0:hw]).then_inc(sem["cp%d" % h], 1)
+    for h in range(HALVES):
+        q = g.sync if h % 2 == 0 else g.scalar
+        q.wait_ge(sem["cp%d" % h], 1)
+        q.dma_start(T.y[:, h * hw:(h + 1) * hw], T.ysb[:, h * hw:(h + 1) * hw]).then_inc(sem["st%d" % h], 16)
+        q.wait_ge(sem["st%d" % h], 16)

@@ -6,11 +6,8 @@ P, W, M = 128, 512, 128
 NCOL = 4
 NSC = 2
 HALVES = 2
-
-RELAY = "partner"
-SHARE = True
+HW = W // HALVES
 HOME = 8
-CRIT_FIRST = False
 
 SCRATCH = {
     "xs": ("sbuf", [P, W], "bfloat16"),
@@ -25,7 +22,8 @@ for _i in range(NSC):
 for _i in range(HALVES):
     SCRATCH["ps%d" % _i] = ("psum", [P, 512], "float32")
 
-SEMAPHORES = (["xl", "al", "ks", "aw", "sent"] + ["arr%d" % i for i in range(NCOL)]
+SEMAPHORES = (["al", "ks", "aw", "sent"] + ["xl%d" % h for h in range(HALVES)]
+              + ["arr%d_%d" % (i, h) for i in range(NCOL) for h in range(HALVES)]
               + ["mm%d" % i for i in range(HALVES)] + ["cp%d" % i for i in range(HALVES)]
               + ["st%d" % i for i in range(HALVES)])
 
@@ -57,80 +55,61 @@ def _plan(T, topo):
         while c in clash:
             c += 1
         colour[j] = c
-    routes = {}
-    load = {}
-    edges = [(j, r) for r in range(n) for j in need[r]]
-    opts = {}
-    for (j, r) in edges:
-        s, d = cores[j], cores[r]
-        if topo.chip(s) == topo.chip(d):
-            routes[(j, r)] = [s, d]
-            continue
-        o = [s] if topo.may_write(s, d) else []
-        if RELAY == "helper":
-            if not o:
-                o = [h for h in range(SIM_CORES) if h not in group and topo.chip(h) == topo.chip(s)
-                     and topo.die(h) == topo.die(s) and topo.may_write(h, d)]
-        elif SHARE or not o:
-            o += [cores[q] for q in range(n) if j in need[q] and topo.chip(cores[q]) == topo.chip(s)
-                  and topo.may_write(cores[q], d)]
-        opts[(j, r)] = o
-    for e in sorted(opts, key=lambda e: (len(opts[e]) > 1 and RELAY != "helper", e)):
-        s, d = cores[e[0]], cores[e[1]]
-        h = min(opts[e], key=lambda c: (load.get(c, 0), c != s, c))
-        load[h] = load.get(h, 0) + 1
-        routes[e] = [s, d] if h == s else [s, h, d]
-    hops = {e: len(p) - 1 for e, p in routes.items()}
-    own, fwd = {}, {}
-    for (j, r), p in routes.items():
-        lst = own.setdefault(p[0], [])
-        hit = [t for t in lst if t[0] == p[1]]
-        if not hit:
-            hit = [[p[1], j, False]]
-            lst.append(hit[0])
-        if len(p) > 2:
-            hit[0][2] = True
-            fwd.setdefault(p[1], {}).setdefault(j, []).append(p[2])
-    calls = {}
-    for c, lst in own.items():
-        if CRIT_FIRST:
-            parts = [[t for t in lst if t[2]], [t for t in lst if not t[2]]]
+    calls, late, when, taken = {}, {}, {}, set()
+    for j in range(n):
+        s = cores[j]
+        tos = [cores[r] for r in range(n) if j in need[r]]
+        near = [d for d in tos if topo.chip(d) == topo.chip(s)]
+        direct = [d for d in tos if topo.chip(d) != topo.chip(s) and topo.may_write(s, d)]
+        blocked = [d for d in tos if topo.chip(d) != topo.chip(s) and not topo.may_write(s, d)]
+        aides = []
+        for d in blocked:
+            h = [k for k in range(SIM_CORES) if k not in group and k not in taken and topo.chip(k) == topo.chip(s)
+                 and topo.die(k) == topo.die(s) and topo.may_write(k, d)][0]
+            taken.add(h)
+            aides.append(h)
+            calls[h] = [("arr", j, 0, [d])]
+            when[(d, j, 0)] = 2.5
+            q = [k for k in near if topo.may_write(k, d)][0]
+            late.setdefault(q, {}).setdefault(j, []).append(d)
+            when[(d, j, 1)] = 3.5
+        if blocked:
+            mine = [("x", j, 0, aides + direct), ("x", j, 1, near + direct), ("x", j, 0, near)]
         else:
-            parts = [sorted(lst, key=lambda t: not t[2])]
-        for part in parts:
-            if part:
-                calls.setdefault(c, []).append(("x", part[0][1], [t[0] for t in part]))
-    for c, by in fwd.items():
+            mine = [("x", j, h, near + direct) for h in range(HALVES)]
+        calls[s] = mine
+        for i, (_k, _j, piece, ds) in enumerate(mine):
+            for d in ds:
+                when[(d, j, piece)] = i + (0.5 if topo.chip(d) != topo.chip(s) else 0.0)
+    for q, by in late.items():
         for j in sorted(by):
-            calls.setdefault(c, []).append(("arr", j, by[j]))
-    far = {c: [d for d in cores if topo.chip(d) != topo.chip(c)][0] for c in calls}
+            calls[q].append(("arr", j, 1, by[j]))
     out, income = {}, {}
     for c, cl in calls.items():
-        lo = _bits(topo.mask(c, far[c]))
-        leaves = any(topo.chip(d) != topo.chip(c) for _k, _j, tos in cl for d in tos)
+        lo = _bits(topo.mask(c, [d for d in cores if topo.chip(d) != topo.chip(c)][0]))
+        every = _bits(topo.mask(c, [k for k in range(SIM_CORES) if k != c and topo.chip(k) == topo.chip(c)][0]))
+        leaves = any(topo.chip(d) != topo.chip(c) for _k, _j, _p, tos in cl for d in tos)
+        pool = lo if leaves else every[0::len(every) // HOME]
         out[c] = []
-        for kind, j, tos in cl:
+        for kind, j, piece, tos in cl:
             near = [d for d in tos if topo.chip(d) == topo.chip(c)]
             away = [d for d in tos if topo.chip(d) != topo.chip(c)]
-            if not leaves:
-                every = _bits(topo.mask(c, near[0]))
-                give = dict(zip(tos, _deal(every[0::len(every) // HOME], len(tos))))
-            elif len(tos) <= 2 or not near:
-                give = dict(zip(tos, _deal(lo, len(tos))))
+            if len(tos) <= 2 or not near or not away:
+                give = dict(zip(tos, _deal(pool, len(tos))))
             else:
-                hi = [b for b in _bits(topo.mask(c, near[0])) if b not in lo]
+                hi = [b for b in every if b not in lo]
                 give = dict(zip(away, _deal(lo, len(away))))
                 give.update(zip(near, _deal(hi[0::2], len(near))))
             trs = []
             for d in tos:
                 trs.append((d, sum(1 << b for b in give[d]), len(give[d])))
-                income[(d, j)] = len(give[d])
-            out[c].append((kind, j, trs))
-    return need, colour, hops, out, income
+                income[(d, j, piece)] = len(give[d])
+            out[c].append((kind, j, piece, trs))
+    return need, colour, when, out, income
 
 
 def rank_program(g, core, T, topo):
-    need, colour, hops, calls, income = _plan(T, topo)
+    need, colour, when, calls, income = _plan(T, topo)
     rank = T.rank_of(core)
     mine = calls.get(core, [])
     if rank is None and not mine:
@@ -138,23 +117,26 @@ def rank_program(g, core, T, topo):
     sem = T.sem
 
     if rank is not None:
-        g.sync.dma_start(T.xs[:, :], T.x[:, :]).then_inc(sem.xl, 16)
+        for h in range(HALVES):
+            g.sync.dma_start(T.xs[:, h * HW:(h + 1) * HW], T.x[:, h * HW:(h + 1) * HW]).then_inc(sem["xl%d" % h], 16)
         g.sync.dma_start(T.a1[:, :], T.a[:, :]).then_inc(sem.al, 16)
 
     sent = 0
-    for kind, j, trs in mine:
+    for kind, j, piece, trs in mine:
         col = colour[j]
+        arr = sem["arr%d_%d" % (col, piece)]
+        lo, hi = piece * HW, (piece + 1) * HW
         if kind == "x":
-            g.wait_ge(sem.xl, 16)
-            src = T.xs[:, :]
+            g.wait_ge(sem["xl%d" % piece], 16)
+            src = T.xs[:, lo:hi]
         else:
-            g.wait_ge(sem["arr%d" % col], income[(core, j)])
-            src = T["land%d" % col][:, :]
+            g.wait_ge(arr, income[(core, j, piece)])
+            src = T["land%d" % col][:, lo:hi]
         lst = []
         for d, mask, cnt in trs:
             rid, pid, _se = topo.addr(d)
             lst.append(RemoteDMATransfer(dst_ids=[DstId(rid=rid, pnc=pid)], dma_engine_mask=mask,
-                                         remote_sem=sem["arr%d" % col], src=src, dst=T["land%d" % col][:, :]))
+                                         remote_sem=arr, src=src, dst=T["land%d" % col][:, lo:hi]))
             sent += cnt
         g.remote_dma_fused(lst, local_sem=sem.sent)
     if sent:
@@ -175,30 +157,29 @@ def rank_program(g, core, T, topo):
             g.vector.tensor_tensor(T["as%d" % i][:, :], T.a1[:, :], T["kc%d" % i][:, :],
                                    AluOpType.mult).then_inc(sem.aw, 1)
 
-    order = sorted(need[rank], key=lambda j: (hops[(j, rank)], topo.chip(T.cores[j]) != topo.chip(core),
-                                              -income[(core, j)], j))
-    hw = W // HALVES
+    order = sorted([(j, h) for j in need[rank] for h in range(HALVES)], key=lambda e: (when[(core, e[0], e[1])], e))
+    left = {h: len(need[rank]) for h in range(HALVES)}
     g.tensor.wait_ge(sem.al, 16)
     if vals:
         g.tensor.wait_ge(sem.aw, len(vals))
-    g.tensor.wait_ge(sem.xl, 16)
-    for k, j in enumerate([rank] + order):
-        if j == rank:
-            blk = T.xs
-        else:
-            blk = T["land%d" % colour[j]]
-            g.tensor.wait_ge(sem["arr%d" % colour[j]], income[(core, j)])
-        last = k == len(order)
-        for h in range(HALVES):
-            mm = g.tensor.matmul(T["ps%d" % h][:, 0:hw], lhs[row[j]][:, :], blk[:, h * hw:(h + 1) * hw], k == 0, last)
-            if last:
-                mm.then_inc(sem["mm%d" % h], 1)
+    for h in range(HALVES):
+        g.tensor.wait_ge(sem["xl%d" % h], 16)
+        g.tensor.matmul(T["ps%d" % h][:, 0:HW], lhs[row[rank]][:, :], T.xs[:, h * HW:(h + 1) * HW], True, False)
+    for j, h in order:
+        g.tensor.wait_ge(sem["arr%d_%d" % (colour[j], h)], income[(core, j, h)])
+        left[h] -= 1
+        mm = g.tensor.matmul(T["ps%d" % h][:, 0:HW], lhs[row[j]][:, :], T["land%d" % colour[j]][:, h * HW:(h + 1) * HW],
+                             False, left[h] == 0)
+        if left[h] == 0:
+            mm.then_inc(sem["mm%d" % h], 1)
 
-    for h in range(HALVES):
+    done = [h for _j, h in order]
+    fin = sorted(range(HALVES), key=lambda h: max(i for i, v in enumerate(done) if v == h))
+    for h in fin:
         g.vector.wait_ge(sem["mm%d" % h], 1)
-        g.vector.tensor_copy(T.ysb[:, h * hw:(h + 1) * hw], T["ps%d" % h][:, 0:hw]).then_inc(sem["cp%d" % h], 1)
-    for h in range(HALVES):
-        q = g.sync if h % 2 == 0 else g.scalar
+        g.vector.tensor_copy(T.ysb[:, h * HW:(h + 1) * HW], T["ps%d" % h][:, 0:HW]).then_inc(sem["cp%d" % h], 1)
+    for i, h in enumerate(fin):
+        q = g.sync if i % 2 == 0 else g.scalar
         q.wait_ge(sem["cp%d" % h], 1)
-        q.dma_start(T.y[:, h * hw:(h + 1) * hw], T.ysb[:, h * hw:(h + 1) * hw]).then_inc(sem["st%d" % h], 16)
+        q.dma_start(T.y[:, h * HW:(h + 1) * HW], T.ysb[:, h * HW:(h + 1) * HW]).then_inc(sem["st%d" % h], 16)
         q.wait_ge(sem["st%d" % h], 16)

@@ -5,9 +5,9 @@ SIM_CORES = 112
 P, W, M = 128, 512, 128
 NCOL = 4
 NSC = 2
-HALVES = 2
-HW = W // HALVES
-HOME = 8
+SPANS = [(0, 128), (128, 320), (320, 512), (0, 320), (128, 512), (0, 512)]
+COVERS = [[0], [1], [2], [0, 1], [1, 2], [0, 1, 2]]
+NP = 3
 
 SCRATCH = {
     "xs": ("sbuf", [P, W], "bfloat16"),
@@ -19,13 +19,13 @@ for _i in range(NCOL):
 for _i in range(NSC):
     SCRATCH["kc%d" % _i] = ("sbuf", [P, M], "bfloat16")
     SCRATCH["as%d" % _i] = ("sbuf", [P, M], "bfloat16")
-for _i in range(HALVES):
+for _i in range(NP):
     SCRATCH["ps%d" % _i] = ("psum", [P, 512], "float32")
 
-SEMAPHORES = (["al", "ks", "aw", "sent"] + ["xl%d" % h for h in range(HALVES)]
-              + ["arr%d_%d" % (i, h) for i in range(NCOL) for h in range(HALVES)]
-              + ["mm%d" % i for i in range(HALVES)] + ["cp%d" % i for i in range(HALVES)]
-              + ["st%d" % i for i in range(HALVES)])
+SEMAPHORES = (["al", "ks", "aw", "sent"] + ["xl%d" % h for h in range(NP)]
+              + ["arr%d_%d" % (i, h) for i in range(NCOL) for h in range(len(SPANS))]
+              + ["mm%d" % i for i in range(NP)] + ["cp%d" % i for i in range(NP)]
+              + ["st%d" % i for i in range(NP)])
 
 
 def _bits(mask):
@@ -55,7 +55,7 @@ def _plan(T, topo):
         while c in clash:
             c += 1
         colour[j] = c
-    calls, late, when, taken = {}, {}, {}, set()
+    calls, late, when, via, taken, handers = {}, {}, {}, {}, set(), set()
     for j in range(n):
         s = cores[j]
         tos = [cores[r] for r in range(n) if j in need[r]]
@@ -68,48 +68,57 @@ def _plan(T, topo):
                  and topo.die(k) == topo.die(s) and topo.may_write(k, d)][0]
             taken.add(h)
             aides.append(h)
-            calls[h] = [("arr", j, 0, [d])]
-            when[(d, j, 0)] = 2.5
+            calls[h] = [("arr", j, 0, [d]), ("arr", j, 1, [d])]
+            when[(d, j, 0)], via[(d, j, 0)] = 3.6, 0
+            when[(d, j, 1)], via[(d, j, 1)] = 4.2, 1
             q = [k for k in near if topo.may_write(k, d)][0]
             late.setdefault(q, {}).setdefault(j, []).append(d)
-            when[(d, j, 1)] = 3.5
+            when[(d, j, 2)], via[(d, j, 2)] = 5.0, 2
         if blocked:
-            mine = [("x", j, 0, aides + direct), ("x", j, 1, near + direct), ("x", j, 0, near)]
+            handers.add(s)
+            mine = [("x", j, 0, aides), ("x", j, 1, aides), ("x", j, 2, near)]
+            if direct:
+                mine.append(("x", j, 5, direct))
+            mine.append(("x", j, 3, near))
         else:
-            mine = [("x", j, h, near + direct) for h in range(HALVES)]
+            mine = [("x", j, 0, direct), ("x", j, 4, near + direct), ("x", j, 0, near)]
         calls[s] = mine
-        for i, (_k, _j, piece, ds) in enumerate(mine):
+        for i, (_k, _j, span, ds) in enumerate(mine):
             for d in ds:
-                when[(d, j, piece)] = i + (0.5 if topo.chip(d) != topo.chip(s) else 0.0)
+                for piece in COVERS[span]:
+                    t = i + (0.5 if topo.chip(d) != topo.chip(s) else 0.0) + len(COVERS[span]) - 1
+                    when[(d, j, piece)] = min(t, 3.5)
+                    via[(d, j, piece)] = span
     for q, by in late.items():
         for j in sorted(by):
-            calls[q].append(("arr", j, 1, by[j]))
+            calls[q].append(("arr", j, 2, by[j]))
     out, income = {}, {}
     for c, cl in calls.items():
         lo = _bits(topo.mask(c, [d for d in cores if topo.chip(d) != topo.chip(c)][0]))
         every = _bits(topo.mask(c, [k for k in range(SIM_CORES) if k != c and topo.chip(k) == topo.chip(c)][0]))
-        leaves = any(topo.chip(d) != topo.chip(c) for _k, _j, _p, tos in cl for d in tos)
-        pool = lo if leaves else every[0::len(every) // HOME]
+        hi = [b for b in every if b not in lo]
+        home = lambda d: topo.chip(d) == topo.chip(c)
+        leaves = any(not home(d) for _k, _j, _p, tos in cl for d in tos)
         out[c] = []
-        for kind, j, piece, tos in cl:
-            near = [d for d in tos if topo.chip(d) == topo.chip(c)]
-            away = [d for d in tos if topo.chip(d) != topo.chip(c)]
-            if len(tos) <= 2 or not near or not away:
-                give = dict(zip(tos, _deal(pool, len(tos))))
-            else:
-                hi = [b for b in every if b not in lo]
-                give = dict(zip(away, _deal(lo, len(away))))
-                give.update(zip(near, _deal(hi[0::2], len(near))))
+        for kind, j, span, tos in cl:
+            near = [d for d in tos if home(d)]
+            away = [d for d in tos if not home(d)]
+            give = {}
+            if near:
+                pool = (hi if leaves else every) if c in handers else hi[0::2]
+                give.update(zip(near, _deal(pool, len(near))))
+            if away:
+                give.update(zip(away, _deal(lo, len(away))))
             trs = []
             for d in tos:
                 trs.append((d, sum(1 << b for b in give[d]), len(give[d])))
-                income[(d, j, piece)] = len(give[d])
-            out[c].append((kind, j, piece, trs))
-    return need, colour, when, out, income
+                income[(d, j, span)] = len(give[d])
+            out[c].append((kind, j, span, trs))
+    return need, colour, when, via, out, income
 
 
 def rank_program(g, core, T, topo):
-    need, colour, when, calls, income = _plan(T, topo)
+    need, colour, when, via, calls, income = _plan(T, topo)
     rank = T.rank_of(core)
     mine = calls.get(core, [])
     if rank is None and not mine:
@@ -117,20 +126,23 @@ def rank_program(g, core, T, topo):
     sem = T.sem
 
     if rank is not None:
-        for h in range(HALVES):
-            g.sync.dma_start(T.xs[:, h * HW:(h + 1) * HW], T.x[:, h * HW:(h + 1) * HW]).then_inc(sem["xl%d" % h], 16)
-        g.sync.dma_start(T.a1[:, :], T.a[:, :]).then_inc(sem.al, 16)
+        for h in range(NP):
+            lo, hi = SPANS[h]
+            q = g.sync if h % 2 == 0 else g.scalar
+            q.dma_start(T.xs[:, lo:hi], T.x[:, lo:hi]).then_inc(sem["xl%d" % h], 16)
+        g.scalar.dma_start(T.a1[:, :], T.a[:, :]).then_inc(sem.al, 16)
 
     sent = 0
-    for kind, j, piece, trs in mine:
+    for kind, j, span, trs in mine:
         col = colour[j]
-        arr = sem["arr%d_%d" % (col, piece)]
-        lo, hi = piece * HW, (piece + 1) * HW
+        arr = sem["arr%d_%d" % (col, span)]
+        lo, hi = SPANS[span]
         if kind == "x":
-            g.wait_ge(sem["xl%d" % piece], 16)
+            for piece in COVERS[span]:
+                g.wait_ge(sem["xl%d" % piece], 16)
             src = T.xs[:, lo:hi]
         else:
-            g.wait_ge(arr, income[(core, j, piece)])
+            g.wait_ge(arr, income[(core, j, span)])
             src = T["land%d" % col][:, lo:hi]
         lst = []
         for d, mask, cnt in trs:
@@ -157,29 +169,36 @@ def rank_program(g, core, T, topo):
             g.vector.tensor_tensor(T["as%d" % i][:, :], T.a1[:, :], T["kc%d" % i][:, :],
                                    AluOpType.mult).then_inc(sem.aw, 1)
 
-    order = sorted([(j, h) for j in need[rank] for h in range(HALVES)], key=lambda e: (when[(core, e[0], e[1])], e))
-    left = {h: len(need[rank]) for h in range(HALVES)}
+    order = sorted([(j, h) for j in need[rank] for h in range(NP)], key=lambda e: (when[(core, e[0], e[1])], e))
+    left = {h: len(need[rank]) for h in range(NP)}
     g.tensor.wait_ge(sem.al, 16)
     if vals:
         g.tensor.wait_ge(sem.aw, len(vals))
-    for h in range(HALVES):
+    for h in range(NP):
+        lo, hi = SPANS[h]
         g.tensor.wait_ge(sem["xl%d" % h], 16)
-        g.tensor.matmul(T["ps%d" % h][:, 0:HW], lhs[row[rank]][:, :], T.xs[:, h * HW:(h + 1) * HW], True, False)
+        g.tensor.matmul(T["ps%d" % h][:, 0:hi - lo], lhs[row[rank]][:, :], T.xs[:, lo:hi], True, False)
     for j, h in order:
-        g.tensor.wait_ge(sem["arr%d_%d" % (colour[j], h)], income[(core, j, h)])
+        lo, hi = SPANS[h]
+        span = via[(core, j, h)]
+        g.tensor.wait_ge(sem["arr%d_%d" % (colour[j], span)], income[(core, j, span)])
         left[h] -= 1
-        mm = g.tensor.matmul(T["ps%d" % h][:, 0:HW], lhs[row[j]][:, :], T["land%d" % colour[j]][:, h * HW:(h + 1) * HW],
+        mm = g.tensor.matmul(T["ps%d" % h][:, 0:hi - lo], lhs[row[j]][:, :], T["land%d" % colour[j]][:, lo:hi],
                              False, left[h] == 0)
         if left[h] == 0:
             mm.then_inc(sem["mm%d" % h], 1)
 
     done = [h for _j, h in order]
-    fin = sorted(range(HALVES), key=lambda h: max(i for i, v in enumerate(done) if v == h))
+    fin = sorted(range(NP), key=lambda h: max(i for i, v in enumerate(done) if v == h))
     for h in fin:
+        lo, hi = SPANS[h]
         g.vector.wait_ge(sem["mm%d" % h], 1)
-        g.vector.tensor_copy(T.ysb[:, h * HW:(h + 1) * HW], T["ps%d" % h][:, 0:HW]).then_inc(sem["cp%d" % h], 1)
+        g.vector.tensor_copy(T.ysb[:, lo:hi], T["ps%d" % h][:, 0:hi - lo]).then_inc(sem["cp%d" % h], 1)
     for i, h in enumerate(fin):
+        lo, hi = SPANS[h]
         q = g.sync if i % 2 == 0 else g.scalar
         q.wait_ge(sem["cp%d" % h], 1)
-        q.dma_start(T.y[:, h * HW:(h + 1) * HW], T.ysb[:, h * HW:(h + 1) * HW]).then_inc(sem["st%d" % h], 16)
+        q.dma_start(T.y[:, lo:hi], T.ysb[:, lo:hi]).then_inc(sem["st%d" % h], 16)
+    for i, h in enumerate(fin):
+        q = g.sync if i % 2 == 0 else g.scalar
         q.wait_ge(sem["st%d" % h], 16)

from concourse.bass import DstId, RemoteDMATransfer
from concourse.mybir import AluOpType

SIM_CORES = 112
P, W, M = 128, 512, 128
NCOL = 4
NSC = 2
SPANS = [(0, 128), (128, 320), (320, 512), (0, 320), (128, 512), (0, 512)]
COVERS = [[0], [1], [2], [0, 1], [1, 2], [0, 1, 2]]
NP = 3

SCRATCH = {
    "xs": ("sbuf", [P, W], "bfloat16"),
    "a1": ("sbuf", [P, M], "bfloat16"),
    "ysb": ("sbuf", [P, W], "bfloat16"),
}
for _i in range(NCOL):
    SCRATCH["land%d" % _i] = ("sbuf", [P, W], "bfloat16")
for _i in range(NSC):
    SCRATCH["kc%d" % _i] = ("sbuf", [P, M], "bfloat16")
    SCRATCH["as%d" % _i] = ("sbuf", [P, M], "bfloat16")
for _i in range(NP):
    SCRATCH["ps%d" % _i] = ("psum", [P, 512], "float32")

SEMAPHORES = (["al", "ks", "aw", "sent"] + ["xl%d" % h for h in range(NP)]
              + ["arr%d_%d" % (i, h) for i in range(NCOL) for h in range(len(SPANS))]
              + ["mm%d" % i for i in range(NP)] + ["cp%d" % i for i in range(NP)]
              + ["st%d" % i for i in range(NP)])


def _bits(mask):
    return [b for b in range(mask.bit_length()) if (mask >> b) & 1]


def _deal(ws, m):
    if m == 1:
        return [ws]
    h = m // 2
    return _deal(ws[0::2], h) + _deal(ws[1::2], m - h)


def _plan(T, topo):
    cores = list(T.cores)
    n = len(cores)
    coef = T.tables["COEF"]
    group = set(cores)
    need = {r: [j for j in range(n) if j != r and coef[r][j] != 0] for r in range(n)}
    colour = {}
    for j in range(n):
        clash = set()
        for r in range(n):
            if j in need[r]:
                clash |= {colour[i] for i in need[r] if i in colour and i != j}
        c = 0
        while c in clash:
            c += 1
        colour[j] = c
    calls, late, when, via, taken, handers = {}, {}, {}, {}, set(), set()
    for j in range(n):
        s = cores[j]
        tos = [cores[r] for r in range(n) if j in need[r]]
        near = [d for d in tos if topo.chip(d) == topo.chip(s)]
        direct = [d for d in tos if topo.chip(d) != topo.chip(s) and topo.may_write(s, d)]
        blocked = [d for d in tos if topo.chip(d) != topo.chip(s) and not topo.may_write(s, d)]
        aides = []
        for d in blocked:
            h = [k for k in range(SIM_CORES) if k not in group and k not in taken and topo.chip(k) == topo.chip(s)
                 and topo.die(k) == topo.die(s) and topo.may_write(k, d)][0]
            taken.add(h)
            aides.append(h)
            calls[h] = [("arr", j, 0, [d]), ("arr", j, 1, [d])]
            when[(d, j, 0)], via[(d, j, 0)] = 3.6, 0
            when[(d, j, 1)], via[(d, j, 1)] = 4.2, 1
            q = [k for k in near if topo.may_write(k, d)][0]
            late.setdefault(q, {}).setdefault(j, []).append(d)
            when[(d, j, 2)], via[(d, j, 2)] = 5.0, 2
        if blocked:
            handers.add(s)
            mine = [("x", j, 0, aides), ("x", j, 1, aides), ("x", j, 2, near)]
            if direct:
                mine.append(("x", j, 5, direct))
            mine.append(("x", j, 3, near))
        else:
            mine = [("x", j, 0, direct), ("x", j, 4, near + direct), ("x", j, 0, near)]
        calls[s] = mine
        for i, (_k, _j, span, ds) in enumerate(mine):
            for d in ds:
                for piece in COVERS[span]:
                    t = i + (0.5 if topo.chip(d) != topo.chip(s) else 0.0) + len(COVERS[span]) - 1
                    when[(d, j, piece)] = min(t, 3.5)
                    via[(d, j, piece)] = span
    for q, by in late.items():
        for j in sorted(by):
            calls[q].append(("arr", j, 2, by[j]))
    out, income = {}, {}
    for c, cl in calls.items():
        lo = _bits(topo.mask(c, [d for d in cores if topo.chip(d) != topo.chip(c)][0]))
        every = _bits(topo.mask(c, [k for k in range(SIM_CORES) if k != c and topo.chip(k) == topo.chip(c)][0]))
        hi = [b for b in every if b not in lo]
        home = lambda d: topo.chip(d) == topo.chip(c)
        leaves = any(not home(d) for _k, _j, _p, tos in cl for d in tos)
        out[c] = []
        for kind, j, span, tos in cl:
            near = [d for d in tos if home(d)]
            away = [d for d in tos if not home(d)]
            give = {}
            if near:
                pool = (hi if leaves else every) if c in handers else hi[0::2]
                give.update(zip(near, _deal(pool, len(near))))
            if away:
                give.update(zip(away, _deal(lo, len(away))))
            trs = []
            for d in tos:
                trs.append((d, sum(1 << b for b in give[d]), len(give[d])))
                income[(d, j, span)] = len(give[d])
            out[c].append((kind, j, span, trs))
    return need, colour, when, via, out, income


def rank_program(g, core, T, topo):
    need, colour, when, via, calls, income = _plan(T, topo)
    rank = T.rank_of(core)
    mine = calls.get(core, [])
    if rank is None and not mine:
        return
    sem = T.sem

    if rank is not None:
        for h in range(NP):
            lo, hi = SPANS[h]
            q = g.sync if h % 2 == 0 else g.scalar
            q.dma_start(T.xs[:, lo:hi], T.x[:, lo:hi]).then_inc(sem["xl%d" % h], 16)
        g.scalar.dma_start(T.a1[:, :], T.a[:, :]).then_inc(sem.al, 16)

    sent = 0
    for kind, j, span, trs in mine:
        col = colour[j]
        arr = sem["arr%d_%d" % (col, span)]
        lo, hi = SPANS[span]
        if kind == "x":
            for piece in COVERS[span]:
                g.wait_ge(sem["xl%d" % piece], 16)
            src = T.xs[:, lo:hi]
        else:
            g.wait_ge(arr, income[(core, j, span)])
            src = T["land%d" % col][:, lo:hi]
        lst = []
        for d, mask, cnt in trs:
            rid, pid, _se = topo.addr(d)
            lst.append(RemoteDMATransfer(dst_ids=[DstId(rid=rid, pnc=pid)], dma_engine_mask=mask,
                                         remote_sem=arr, src=src, dst=T["land%d" % col][:, lo:hi]))
            sent += cnt
        g.remote_dma_fused(lst, local_sem=sem.sent)
    if sent:
        g.wait_ge(sem.sent, sent)
    if rank is None:
        return

    row = T.tables["COEF"][rank]
    vals = sorted({row[j] for j in need[rank] + [rank]} - {1})
    lhs = {1: T.a1}
    for i, c in enumerate(vals):
        g.vector.memset(T["kc%d" % i][:, :], float(c)).then_inc(sem.ks, 1)
        lhs[c] = T["as%d" % i]
    if vals:
        g.vector.wait_ge(sem.ks, len(vals))
        g.vector.wait_ge(sem.al, 16)
        for i, c in enumerate(vals):
            g.vector.tensor_tensor(T["as%d" % i][:, :], T.a1[:, :], T["kc%d" % i][:, :],
                                   AluOpType.mult).then_inc(sem.aw, 1)

    order = sorted([(j, h) for j in need[rank] for h in range(NP)], key=lambda e: (when[(core, e[0], e[1])], e))
    left = {h: len(need[rank]) for h in range(NP)}
    g.tensor.wait_ge(sem.al, 16)
    if vals:
        g.tensor.wait_ge(sem.aw, len(vals))
    for h in range(NP):
        lo, hi = SPANS[h]
        g.tensor.wait_ge(sem["xl%d" % h], 16)
        g.tensor.matmul(T["ps%d" % h][:, 0:hi - lo], lhs[row[rank]][:, :], T.xs[:, lo:hi], True, False)
    for j, h in order:
        lo, hi = SPANS[h]
        span = via[(core, j, h)]
        g.tensor.wait_ge(sem["arr%d_%d" % (colour[j], span)], income[(core, j, span)])
        left[h] -= 1
        mm = g.tensor.matmul(T["ps%d" % h][:, 0:hi - lo], lhs[row[j]][:, :], T["land%d" % colour[j]][:, lo:hi],
                             False, left[h] == 0)
        if left[h] == 0:
            mm.then_inc(sem["mm%d" % h], 1)

    done = [h for _j, h in order]
    fin = sorted(range(NP), key=lambda h: max(i for i, v in enumerate(done) if v == h))
    for h in fin:
        lo, hi = SPANS[h]
        g.vector.wait_ge(sem["mm%d" % h], 1)
        g.vector.tensor_copy(T.ysb[:, lo:hi], T["ps%d" % h][:, 0:hi - lo]).then_inc(sem["cp%d" % h], 1)
    for i, h in enumerate(fin):
        lo, hi = SPANS[h]
        q = g.sync if i % 2 == 0 else g.scalar
        q.wait_ge(sem["cp%d" % h], 1)
        q.dma_start(T.y[:, lo:hi], T.ysb[:, lo:hi]).then_inc(sem["st%d" % h], 16)
    for i, h in enumerate(fin):
        q = g.sync if i % 2 == 0 else g.scalar
        q.wait_ge(sem["st%d" % h], 16)
